import numpy as np
import ml_dtypes


def mxq(x, axis, fmt="e4m3"):
    dtype, down = {"e4m3": (ml_dtypes.float8_e4m3fn, 7), "e5m2": (ml_dtypes.float8_e5m2, 14)}[fmt]
    v = np.moveaxis(np.asarray(x, np.float32).astype(ml_dtypes.bfloat16).astype(np.float64), axis, -1)
    blocks = v.reshape(v.shape[:-1] + (-1, 32))
    amax = np.abs(blocks).max(-1, keepdims=True)
    byte = np.maximum(np.where(amax > 0, np.frexp(amax)[1] - 1 + 127, 0) - down, 1)
    scale = np.exp2(byte - 127.0)
    codes = (blocks / scale).astype(np.float32).astype(dtype).astype(np.float64)
    return np.moveaxis((codes * scale).reshape(v.shape), -1, axis)


WIDE = False


def mx_kscale(k):
    if not WIDE:
        return np.ones(k)
    levels = np.array([10, -10, 5, -5, 0])
    if k % 512:
        return np.exp2(np.random.permutation(np.resize(levels, k // 32))).repeat(32)
    a = np.empty((k // 512, 16))
    for p in range(k // 512):
        a[p, :8] = np.random.permutation(np.resize(levels, 8))
        for g in range(8):
            far = levels[np.abs(levels - a[p, g]) >= 10]
            a[p, g + 8] = far[np.random.randint(len(far))]
    return np.exp2(a.ravel()).repeat(32)


def f64(x):
    return np.asarray(x).astype(np.float64)


def striped(idx):
    return np.tile(idx.reshape(-1, 16).T, (8, 1)).astype(np.uint16)


def unstriped(offs):
    return offs[:16].T.reshape(-1).astype(np.int64)


def pack_weight(w):
    k, n = w.shape
    w = f64(np.asarray(w, np.float32).astype(ml_dtypes.bfloat16)).reshape(k // 32, 32, n)
    amax = np.abs(w).max(1)
    byte = np.clip(np.where(amax > 0, np.frexp(amax)[1] - 1 + 127 - 7, 1), 1, 254)
    scaled = (w * np.exp2(127.0 - byte)[:, None, :]).reshape(k, n).astype(np.float32)
    words = np.ascontiguousarray(scaled.reshape(k // 512, 128, 4, n).transpose(0, 1, 3, 2)).astype(ml_dtypes.float8_e4m3fn).view(np.uint8)
    return words, np.ascontiguousarray(byte.astype(np.uint8).reshape(k // 512, 16, n))


def unpack_weight(words, scales):
    g, p, n, _ = words.shape
    vals = np.ascontiguousarray(words).view(ml_dtypes.float8_e4m3fn).astype(np.float64) * np.repeat(np.exp2(scales.astype(np.float64) - 127.0), 8, axis=1)[..., None]
    return vals.transpose(0, 1, 3, 2).reshape(g * 512, n)


K, T, S, N, H, U = 1024, 2048, 512, 128, 512, 1024


def setup_inputs():
    n = np.random.standard_normal
    s = mx_kscale(K)[:, None]
    u = mx_kscale(H)
    packed_xT = pack_weight(n((K, T)) * s)
    return {
        "x_words": packed_xT[0],
        "x_scales": packed_xT[1],
        "w1": (n((K, H)) / np.sqrt(K) / s).astype(np.float32),
        "nl": (np.random.uniform(0.0, 0.6, (H, U))).astype(np.float32),
        "unit": (np.random.uniform(0.6, 1.4, (H, 1)) * u[:, None]).astype(np.float32),
        "w2": (n((H, N)) / np.sqrt(H) / u[:, None]).astype(np.float32),
        "offs": striped(np.random.permutation(T)[:S]),
        "e1": striped(np.random.permutation(np.concatenate([np.arange(S), np.random.randint(0, S, U - S)]))),
        "e2": striped(np.random.permutation(np.concatenate([np.arange(S), np.random.randint(0, S, U - S)]))),
    }


def reference(x_words, x_scales, w1, nl, unit, w2, offs, e1, e2):
    xq = unpack_weight(x_words, x_scales)[:, unstriped(offs)]
    y = mxq(f64(w1), 0, "e4m3").T @ xq
    y1 = y[:, unstriped(e1)]
    y2 = y[:, unstriped(e2)]
    lin = y1 + y2
    bil = y1 * y2
    hid = f64(unit) * (lin + bil * f64(nl))
    return mxq(f64(w2), 0, "e4m3").T @ mxq(hid, 0, "e4m3")

@@ -1,0 +1,201 @@
+from contextlib import ExitStack
+
+import concourse.mybir as mybir
+
+K, T, S, N, H, U = 1024, 2048, 512, 128, 512, 1024
+FLOPS = 2 * K * H * S + 2 * H * N * U
+
+F32 = mybir.dt.float32
+BF16 = mybir.dt.bfloat16
+I32 = mybir.dt.int32
+U32 = mybir.dt.uint32
+U16 = mybir.dt.uint16
+U8 = mybir.dt.uint8
+FP8X4 = mybir.dt.float8_e4m3fn_x4
+MULT = mybir.AluOpType.mult
+ADD = mybir.AluOpType.add
+COPY = mybir.ActivationFunctionType.Copy
+
+P = 128
+PACK = 4
+K_PASS = P * PACK
+PASSES = K // K_PASS
+LIST_ROWS = 16
+CHUNKS = [256, 256, 256, 128, 128]
+
+
+def tile_picked_yspecmx_bil_p_kernel(
+    tc, x_words, x_scales, w1, nl, unit, w2, offs, e1, e2, out
+):
+    nc = tc.nc
+    with ExitStack() as ctx:
+        keep = ctx.enter_context(tc.tile_pool(name="keep", bufs=1))
+        ring = ctx.enter_context(tc.tile_pool(name="ring", bufs=2))
+        psum = ctx.enter_context(tc.psum_pool(name="psum", bufs=1))
+        psum_out = ctx.enter_context(tc.psum_pool(name="psum_out", bufs=2))
+
+        offs_sb = keep.tile([P, S // LIST_ROWS], U16, name="offs_sb")
+        e1_sb = keep.tile([P, U // LIST_ROWS], U16, name="e1_sb")
+        e2_sb = keep.tile([P, U // LIST_ROWS], U16, name="e2_sb")
+
+        scale_table = keep.tile([P, T], U8, name="scale_table", align_bytes=64)
+        nc.vector.memset(scale_table[:].bitcast(I32), 0)
+        for q in range(4):
+            nc.gpsimd.dma_start(
+                out=scale_table[32 * q : 32 * q + 4 * PASSES, :].bitcast(I32),
+                in_=x_scales[:, 4 * q : 4 * q + 4, :].bitcast(I32),
+            )
+
+        nc.sync.dma_start(offs_sb[:], offs)
+        w1_raw = []
+        for o in range(PASSES):
+            raw = keep.tile([P, PACK, H], F32, name=f"w1_raw{o}")
+            nc.sync.dma_start(
+                out=raw[:], in_=w1[o * K_PASS : (o + 1) * K_PASS, :].rearrange("(p j) c -> p j c", j=PACK)
+            )
+            w1_raw.append(raw)
+        word_table = []
+        for o in range(PASSES):
+            table = keep.tile([P, T], I32, name=f"word_table{o}", align_bytes=64)
+            nc.sync.dma_start(out=table[:], in_=x_words[o].rearrange("p n t -> p (n t)").bitcast(I32))
+            word_table.append(table)
+        nc.sync.dma_start(e2_sb[:], e2)
+        nc.sync.dma_start(e1_sb[:], e1)
+        unit_sb = keep.tile([P, PACK], F32, name="unit_sb")
+        nc.sync.dma_start(out=unit_sb[:], in_=unit.rearrange("(p t) o -> p (t o)", t=PACK))
+        w2_raw = keep.tile([P, PACK, N], F32, name="w2_raw")
+        nc.sync.dma_start(out=w2_raw[:], in_=w2.rearrange("(p j) n -> p j n", j=PACK))
+        starts = [sum(CHUNKS[:c]) for c in range(len(CHUNKS))]
+        nl_rows = nl.rearrange("(p t) r -> p t r", t=PACK)
+        nl_sb = []
+        for c, width in enumerate(CHUNKS):
+            share = keep.tile([P, PACK, width], F32, name=f"nl{c}")
+            nc.sync.dma_start(out=share[:], in_=nl_rows[:, :, starts[c] : starts[c] + width])
+            nl_sb.append(share)
+
+        w1_codes, w1_scales = [], []
+        for o in range(PASSES):
+            grouped = keep.tile([P, PACK * H], BF16, name=f"w1_grouped{o}", align_bytes=64)
+            dst = grouped[:].rearrange("p (t m j) -> p m t j", t=PACK, j=PACK)
+            src = w1_raw[o][:].rearrange("p j (m t) -> p m t j", t=PACK)
+            if o == 0:
+                nc.scalar.copy(out=dst, in_=src)
+            else:
+                nc.vector.tensor_copy(out=dst, in_=src)
+            codes = keep.tile([P, H], U32, name=f"w1_codes{o}", align_bytes=64)
+            scales = keep.tile([P, H], U8, name=f"w1_scales{o}", align_bytes=64)
+            nc.vector.quantize_mx(out=codes[:].bitcast(FP8X4), scales=scales[:], in_=grouped[:])
+            w1_codes.append(codes)
+            w1_scales.append(scales)
+
+        x_scale = keep.tile([P, S], U8, name="x_scale", align_bytes=64)
+        nc.vector.tensor_copy(x_scale[:], scale_table[:].indirect(offs_sb[:]))
+
+        banks = [psum.tile([P, S], F32, name=f"y_bank{t}") for t in range(PACK)]
+        pieces = [(0, 0, S), (1, 0, S // 2), (1, S // 2, S)]
+        for n, (o, lo, hi) in enumerate(pieces):
+            picked = keep.tile([P, hi - lo], U32, name=f"x_codes{n}", align_bytes=64)
+            nc.vector.tensor_copy(
+                picked[:], word_table[o][:].bitcast(U32).indirect(offs_sb[:, lo // LIST_ROWS : hi // LIST_ROWS])
+            )
+            for t in range(PACK):
+                nc.tensor.matmul_mx(
+                    out=banks[t][:, lo:hi],
+                    lhsT=w1_codes[o][:, t * P : (t + 1) * P].bitcast(FP8X4),
+                    lhsT_scale=w1_scales[o][:, t * P : (t + 1) * P],
+                    rhs=picked[:].bitcast(FP8X4),
+                    rhs_scale=x_scale[4 * o : P, lo:hi],
+                    start=(n == 0),
+                    stop=(n == len(pieces) - 1),
+                )
+
+        w2_grouped = keep.tile([P, PACK * N], BF16, name="w2_grouped", align_bytes=64)
+        nc.scalar.copy(
+            out=w2_grouped[:].rearrange("p (c i j) -> p c j i", i=4, j=PACK),
+            in_=w2_raw[:].rearrange("p j (c i) -> p c j i", i=4),
+        )
+        w2_codes = keep.tile([P, N], U32, name="w2_codes", align_bytes=64)
+        w2_scales = keep.tile([P, N], U8, name="w2_scales", align_bytes=64)
+
+        y = [keep.tile([P, S], F32, name=f"y{t}") for t in range(PACK)]
+        z = [keep.tile([P, S], F32, name=f"z{t}") for t in range(PACK)]
+        for t in range(PACK):
+            nc.vector.tensor_copy(out=y[t][:], in_=banks[t][:])
+        for t in range(PACK):
+            nc.vector.tensor_scalar(z[t][:], y[t][:], unit_sb[:, t : t + 1], None, MULT)
+        nc.vector.quantize_mx(out=w2_codes[:].bitcast(FP8X4), scales=w2_scales[:], in_=w2_grouped[:])
+
+        def fetch(c):
+            width = CHUNKS[c]
+            cols = slice(starts[c] // LIST_ROWS, (starts[c] + width) // LIST_ROWS)
+            z1 = ring.tile([P, PACK, width], F32, name="z1")
+            y2 = ring.tile([P, PACK, width], F32, name="y2")
+            order = [(t, True) for t in range(PACK)] + [(t, False) for t in range(PACK)]
+            if c > 0:
+                order = [(t, second) for t in range(PACK) for second in (False, True)]
+            for t, second in order:
+                if second:
+                    nc.scalar.activation(y2[:, t, :], y[t][:].indirect(e2_sb[:, cols]), COPY)
+                else:
+                    nc.scalar.activation(z1[:, t, :], z[t][:].indirect(e1_sb[:, cols]), COPY)
+            prod = ring.tile([P, PACK, width], F32, name="prod")
+            rest = ring.tile([P, PACK, width], F32, name="rest")
+            return z1, y2, prod, rest
+
+        def first(c, tiles, t):
+            z1, y2, prod, rest = tiles
+            nc.vector.tensor_tensor(prod[:, t, :], z1[:, t, :], nl_sb[c][:, t, :], MULT)
+
+        def second(c, tiles, t):
+            z1, y2, prod, rest = tiles
+            nc.vector.scalar_tensor_tensor(
+                rest[:, t, :], prod[:, t, :], unit_sb[:, t : t + 1], y2[:, t, :], ADD, MULT
+            )
+
+        def join(c, tiles):
+            z1, y2, prod, rest = tiles
+            hid = ring.tile([P, PACK * CHUNKS[c]], BF16, name="hid", align_bytes=64)
+            nc.vector.tensor_tensor(
+                hid[:].rearrange("p (c i t) -> p c t i", i=4, t=PACK),
+                z1[:].rearrange("p t (c i) -> p c t i", i=4),
+                rest[:].rearrange("p t (c i) -> p c t i", i=4),
+                ADD,
+            )
+            return hid
+
+        def finish(c, hid):
+            width = CHUNKS[c]
+            codes = ring.tile([P, width], U32, name="hid_codes", align_bytes=64)
+            scales = ring.tile([P, width], U8, name="hid_scales", align_bytes=64)
+            nc.vector.quantize_mx(out=codes[:].bitcast(FP8X4), scales=scales[:], in_=hid[:])
+            acc = psum_out.tile([P, width], F32, name="acc")
+            nc.tensor.matmul_mx(
+                out=acc[:],
+                lhsT=w2_codes[:].bitcast(FP8X4),
+                lhsT_scale=w2_scales[:],
+                rhs=codes[:].bitcast(FP8X4),
+                rhs_scale=scales[:],
+                start=True,
+                stop=True,
+            )
+            result = ring.tile([P, width], F32, name="result")
+            nc.scalar.copy(out=result[:], in_=acc[:])
+            nc.sync.dma_start(out=out[:, starts[c] : starts[c] + width], in_=result[:])
+
+        before = None
+        for c in range(len(CHUNKS)):
+            tiles = fetch(c)
+            first(c, tiles, 0)
+            if before is not None:
+                hid = join(c - 1, before)
+            first(c, tiles, 1)
+            if before is not None:
+                finish(c - 1, hid)
+            second(c, tiles, 0)
+            first(c, tiles, 2)
+            second(c, tiles, 1)
+            first(c, tiles, 3)
+            second(c, tiles, 2)
+            second(c, tiles, 3)
+            before = tiles
+        finish(len(CHUNKS) - 1, join(len(CHUNKS) - 1, before))

@@ -30,9 +30,9 @@ def tile_picked_yspecmx_bil_p_kernel(
     nc = tc.nc
     with ExitStack() as ctx:
         keep = ctx.enter_context(tc.tile_pool(name="keep", bufs=1))
-        ring = ctx.enter_context(tc.tile_pool(name="ring", bufs=2))
+        ring = ctx.enter_context(tc.tile_pool(name="ring", bufs=5))
         psum = ctx.enter_context(tc.psum_pool(name="psum", bufs=1))
-        psum_out = ctx.enter_context(tc.psum_pool(name="psum_out", bufs=2))
+        psum_out = ctx.enter_context(tc.psum_pool(name="psum_out", bufs=4))
 
         offs_sb = keep.tile([P, S // LIST_ROWS], U16, name="offs_sb")
         e1_sb = keep.tile([P, U // LIST_ROWS], U16, name="e1_sb")
@@ -40,11 +40,6 @@ def tile_picked_yspecmx_bil_p_kernel(
 
         scale_table = keep.tile([P, T], U8, name="scale_table", align_bytes=64)
         nc.vector.memset(scale_table[:].bitcast(I32), 0)
-        for q in range(4):
-            nc.gpsimd.dma_start(
-                out=scale_table[32 * q : 32 * q + 4 * PASSES, :].bitcast(I32),
-                in_=x_scales[:, 4 * q : 4 * q + 4, :].bitcast(I32),
-            )
 
         nc.sync.dma_start(offs_sb[:], offs)
         w1_raw = []
@@ -54,6 +49,12 @@ def tile_picked_yspecmx_bil_p_kernel(
                 out=raw[:], in_=w1[o * K_PASS : (o + 1) * K_PASS, :].rearrange("(p j) c -> p j c", j=PACK)
             )
             w1_raw.append(raw)
+            if o == 0:
+                for q in range(4):
+                    nc.sync.dma_start(
+                        out=scale_table[32 * q : 32 * q + 4 * PASSES, :].bitcast(I32),
+                        in_=x_scales[:, 4 * q : 4 * q + 4, :].bitcast(I32),
+                    )
         word_table = []
         for o in range(PASSES):
             table = keep.tile([P, T], I32, name=f"word_table{o}", align_bytes=64)
@@ -92,22 +93,27 @@ def tile_picked_yspecmx_bil_p_kernel(
         nc.vector.tensor_copy(x_scale[:], scale_table[:].indirect(offs_sb[:]))
 
         banks = [psum.tile([P, S], F32, name=f"y_bank{t}") for t in range(PACK)]
-        pieces = [(0, 0, S), (1, 0, S // 2), (1, S // 2, S)]
-        for n, (o, lo, hi) in enumerate(pieces):
-            picked = keep.tile([P, hi - lo], U32, name=f"x_codes{n}", align_bytes=64)
-            nc.vector.tensor_copy(
-                picked[:], word_table[o][:].bitcast(U32).indirect(offs_sb[:, lo // LIST_ROWS : hi // LIST_ROWS])
-            )
-            for t in range(PACK):
-                nc.tensor.matmul_mx(
-                    out=banks[t][:, lo:hi],
-                    lhsT=w1_codes[o][:, t * P : (t + 1) * P].bitcast(FP8X4),
-                    lhsT_scale=w1_scales[o][:, t * P : (t + 1) * P],
-                    rhs=picked[:].bitcast(FP8X4),
-                    rhs_scale=x_scale[4 * o : P, lo:hi],
-                    start=(n == 0),
-                    stop=(n == len(pieces) - 1),
+        half = S // 2
+        picked = {}
+        for o in range(PASSES):
+            for h in range(2):
+                picked[o, h] = keep.tile([P, half], U32, name=f"x_codes{o}_{h}", align_bytes=64)
+                nc.vector.tensor_copy(
+                    picked[o, h][:],
+                    word_table[o][:].bitcast(U32).indirect(offs_sb[:, h * half // LIST_ROWS : (h + 1) * half // LIST_ROWS]),
                 )
+        steps = [(0, h, t) for h in range(2) for t in range(PACK)]
+        steps += [(1, h, t) for t0 in (0, 2) for h in range(2) for t in (t0, t0 + 1)]
+        for o, h, t in steps:
+            nc.tensor.matmul_mx(
+                out=banks[t][:, h * half : (h + 1) * half],
+                lhsT=w1_codes[o][:, t * P : (t + 1) * P].bitcast(FP8X4),
+                lhsT_scale=w1_scales[o][:, t * P : (t + 1) * P],
+                rhs=picked[o, h][:].bitcast(FP8X4),
+                rhs_scale=x_scale[4 * o : P, h * half : (h + 1) * half],
+                start=(o == 0 and h == 0),
+                stop=(o == PASSES - 1 and h == 1),
+            )
 
         w2_grouped = keep.tile([P, PACK * N], BF16, name="w2_grouped", align_bytes=64)
         nc.scalar.copy(
@@ -119,9 +125,10 @@ def tile_picked_yspecmx_bil_p_kernel(
 
         y = [keep.tile([P, S], F32, name=f"y{t}") for t in range(PACK)]
         z = [keep.tile([P, S], F32, name=f"z{t}") for t in range(PACK)]
+        nc.scalar.copy(out=y[0][:], in_=banks[0][:])
         for t in range(PACK):
-            nc.vector.tensor_copy(out=y[t][:], in_=banks[t][:])
-        for t in range(PACK):
+            if t + 1 < PACK:
+                nc.vector.tensor_copy(out=y[t + 1][:], in_=banks[t + 1][:])
             nc.vector.tensor_scalar(z[t][:], y[t][:], unit_sb[:, t : t + 1], None, MULT)
         nc.vector.quantize_mx(out=w2_codes[:].bitcast(FP8X4), scales=w2_scales[:], in_=w2_grouped[:])
 
@@ -130,12 +137,14 @@ def tile_picked_yspecmx_bil_p_kernel(
             cols = slice(starts[c] // LIST_ROWS, (starts[c] + width) // LIST_ROWS)
             z1 = ring.tile([P, PACK, width], F32, name="z1")
             y2 = ring.tile([P, PACK, width], F32, name="y2")
-            order = [(t, True) for t in range(PACK)] + [(t, False) for t in range(PACK)]
+            order = [(0, True), (1, True), (0, False), (2, True), (1, False), (3, True), (2, False), (3, False)]
             if c > 0:
                 order = [(t, second) for t in range(PACK) for second in (False, True)]
             for t, second in order:
                 if second:
                     nc.scalar.activation(y2[:, t, :], y[t][:].indirect(e2_sb[:, cols]), COPY)
+                elif c == 0 and t >= 2:
+                    nc.vector.tensor_copy(z1[:, t, :], z[t][:].indirect(e1_sb[:, cols]))
                 else:
                     nc.scalar.activation(z1[:, t, :], z[t][:].indirect(e1_sb[:, cols]), COPY)
             prod = ring.tile([P, PACK, width], F32, name="prod")

@@ -21,7 +21,8 @@ PACK = 4
 K_PASS = P * PACK
 PASSES = K // K_PASS
 LIST_ROWS = 16
-CHUNKS = [256, 256, 256, 128, 128]
+CHUNKS = [256,384,256,128]
+ON_VECTOR = [(0, 3, True), (0, 3, False), (2, 3, True)]
 
 
 def tile_picked_yspecmx_bil_p_kernel(
@@ -30,7 +31,7 @@ def tile_picked_yspecmx_bil_p_kernel(
     nc = tc.nc
     with ExitStack() as ctx:
         keep = ctx.enter_context(tc.tile_pool(name="keep", bufs=1))
-        ring = ctx.enter_context(tc.tile_pool(name="ring", bufs=5))
+        ring = ctx.enter_context(tc.tile_pool(name="ring", bufs=4))
         psum = ctx.enter_context(tc.psum_pool(name="psum", bufs=1))
         psum_out = ctx.enter_context(tc.psum_pool(name="psum_out", bufs=4))
 
@@ -41,7 +42,6 @@ def tile_picked_yspecmx_bil_p_kernel(
         scale_table = keep.tile([P, T], U8, name="scale_table", align_bytes=64)
         nc.vector.memset(scale_table[:].bitcast(I32), 0)
 
-        nc.sync.dma_start(offs_sb[:], offs)
         w1_raw = []
         for o in range(PASSES):
             raw = keep.tile([P, PACK, H], F32, name=f"w1_raw{o}")
@@ -50,6 +50,7 @@ def tile_picked_yspecmx_bil_p_kernel(
             )
             w1_raw.append(raw)
             if o == 0:
+                nc.sync.dma_start(offs_sb[:], offs)
                 for q in range(4):
                     nc.sync.dma_start(
                         out=scale_table[32 * q : 32 * q + 4 * PASSES, :].bitcast(I32),
@@ -70,9 +71,15 @@ def tile_picked_yspecmx_bil_p_kernel(
         nl_rows = nl.rearrange("(p t) r -> p t r", t=PACK)
         nl_sb = []
         for c, width in enumerate(CHUNKS):
-            share = keep.tile([P, PACK, width], F32, name=f"nl{c}")
-            nc.sync.dma_start(out=share[:], in_=nl_rows[:, :, starts[c] : starts[c] + width])
-            nl_sb.append(share)
+            if c == 0:
+                planes = [keep.tile([P, width], F32, name=f"nl0_{t}", tag=f"nl0_{t}") for t in range(PACK)]
+                for t in range(PACK):
+                    nc.sync.dma_start(out=planes[t][:], in_=nl_rows[:, t, :width])
+                nl_sb.append([plane[:] for plane in planes])
+            else:
+                share = keep.tile([P, PACK, width], F32, name=f"nl{c}")
+                nc.sync.dma_start(out=share[:], in_=nl_rows[:, :, starts[c] : starts[c] + width])
+                nl_sb.append([share[:, t, :] for t in range(PACK)])
 
         w1_codes, w1_scales = [], []
         for o in range(PASSES):
@@ -125,35 +132,42 @@ def tile_picked_yspecmx_bil_p_kernel(
 
         y = [keep.tile([P, S], F32, name=f"y{t}") for t in range(PACK)]
         z = [keep.tile([P, S], F32, name=f"z{t}") for t in range(PACK)]
-        nc.scalar.copy(out=y[0][:], in_=banks[0][:])
+        nc.scalar.copy(out=y[0][:, :S], in_=banks[0][:])
         for t in range(PACK):
             if t + 1 < PACK:
-                nc.vector.tensor_copy(out=y[t + 1][:], in_=banks[t + 1][:])
-            nc.vector.tensor_scalar(z[t][:], y[t][:], unit_sb[:, t : t + 1], None, MULT)
+                nc.vector.tensor_copy(out=y[t + 1][:, :S], in_=banks[t + 1][:])
+            nc.gpsimd.tensor_scalar(z[t][:, :S], y[t][:, :S], unit_sb[:, t : t + 1], 0.0, MULT, ADD)
         nc.vector.quantize_mx(out=w2_codes[:].bitcast(FP8X4), scales=w2_scales[:], in_=w2_grouped[:])
+
+        later = keep.tile([P, 2 * PACK * (U - CHUNKS[0])], F32, name="later", tag="nl0_1")
+
+        def look_up(c, z1, y2, t, by_e2):
+            cols = slice(starts[c] // LIST_ROWS, (starts[c] + CHUNKS[c]) // LIST_ROWS)
+            if by_e2:
+                return y2[:, t, :], y[t][:].indirect(e2_sb[:, cols])
+            return z1[:, t, :], z[t][:].indirect(e1_sb[:, cols])
 
         def fetch(c):
             width = CHUNKS[c]
-            cols = slice(starts[c] // LIST_ROWS, (starts[c] + width) // LIST_ROWS)
-            z1 = ring.tile([P, PACK, width], F32, name="z1")
-            y2 = ring.tile([P, PACK, width], F32, name="y2")
-            order = [(0, True), (1, True), (0, False), (2, True), (1, False), (3, True), (2, False), (3, False)]
+            if c == 0:
+                z1 = keep.tile([P, PACK, width], F32, name="z1_first")[:]
+                y2 = keep.tile([P, PACK, width], F32, name="y2_first")[:]
+            else:
+                at = 2 * PACK * (starts[c] - CHUNKS[0])
+                z1 = later[:, at : at + PACK * width].rearrange("p (t r) -> p t r", t=PACK)
+                y2 = later[:, at + PACK * width : at + 2 * PACK * width].rearrange("p (t r) -> p t r", t=PACK)
+            order = [(0, True), (1, True), (0, False), (1, False), (2, True), (2, False), (3, True), (3, False)]
             if c > 0:
                 order = [(t, second) for t in range(PACK) for second in (False, True)]
-            for t, second in order:
-                if second:
-                    nc.scalar.activation(y2[:, t, :], y[t][:].indirect(e2_sb[:, cols]), COPY)
-                elif c == 0 and t >= 2:
-                    nc.vector.tensor_copy(z1[:, t, :], z[t][:].indirect(e1_sb[:, cols]))
-                else:
-                    nc.scalar.activation(z1[:, t, :], z[t][:].indirect(e1_sb[:, cols]), COPY)
-            prod = ring.tile([P, PACK, width], F32, name="prod")
-            rest = ring.tile([P, PACK, width], F32, name="rest")
-            return z1, y2, prod, rest
+            for t, by_e2 in order:
+                if (c, t, by_e2) not in ON_VECTOR:
+                    nc.scalar.activation(*look_up(c, z1, y2, t, by_e2), COPY)
+            prod = keep.tile([P, PACK, width], F32, name="prod")
+            return z1, y2, prod, prod
 
         def first(c, tiles, t):
             z1, y2, prod, rest = tiles
-            nc.vector.tensor_tensor(prod[:, t, :], z1[:, t, :], nl_sb[c][:, t, :], MULT)
+            nc.vector.tensor_tensor(prod[:, t, :], z1[:, t, :], nl_sb[c][t], MULT)
 
         def second(c, tiles, t):
             z1, y2, prod, rest = tiles
@@ -166,7 +180,7 @@ def tile_picked_yspecmx_bil_p_kernel(
             hid = ring.tile([P, PACK * CHUNKS[c]], BF16, name="hid", align_bytes=64)
             nc.vector.tensor_tensor(
                 hid[:].rearrange("p (c i t) -> p c t i", i=4, t=PACK),
-                z1[:].rearrange("p t (c i) -> p c t i", i=4),
+                z1.rearrange("p t (c i) -> p c t i", i=4),
                 rest[:].rearrange("p t (c i) -> p c t i", i=4),
                 ADD,
             )
@@ -178,33 +192,41 @@ def tile_picked_yspecmx_bil_p_kernel(
             scales = ring.tile([P, width], U8, name="hid_scales", align_bytes=64)
             nc.vector.quantize_mx(out=codes[:].bitcast(FP8X4), scales=scales[:], in_=hid[:])
             acc = psum_out.tile([P, width], F32, name="acc")
-            nc.tensor.matmul_mx(
-                out=acc[:],
-                lhsT=w2_codes[:].bitcast(FP8X4),
-                lhsT_scale=w2_scales[:],
-                rhs=codes[:].bitcast(FP8X4),
-                rhs_scale=scales[:],
-                start=True,
-                stop=True,
-            )
+            lo = 0
+            for part in (512, 256, 128):
+                if width - lo >= part:
+                    nc.tensor.matmul_mx(
+                        out=acc[:, lo : lo + part],
+                        lhsT=w2_codes[:].bitcast(FP8X4),
+                        lhsT_scale=w2_scales[:],
+                        rhs=codes[:, lo : lo + part].bitcast(FP8X4),
+                        rhs_scale=scales[:, lo : lo + part],
+                        start=True,
+                        stop=True,
+                    )
+                    lo = lo + part
             result = ring.tile([P, width], F32, name="result")
             nc.scalar.copy(out=result[:], in_=acc[:])
             nc.sync.dma_start(out=out[:, starts[c] : starts[c] + width], in_=result[:])
 
-        before = None
+        hid = None
         for c in range(len(CHUNKS)):
             tiles = fetch(c)
+            for where, t, by_e2 in ON_VECTOR:
+                if where == c and by_e2:
+                    nc.vector.tensor_copy(*look_up(c, tiles[0], tiles[1], t, by_e2))
             first(c, tiles, 0)
-            if before is not None:
-                hid = join(c - 1, before)
-            first(c, tiles, 1)
-            if before is not None:
+            if hid is not None:
                 finish(c - 1, hid)
+            first(c, tiles, 1)
             second(c, tiles, 0)
+            for where, t, by_e2 in ON_VECTOR:
+                if where == c and not by_e2:
+                    nc.vector.tensor_copy(*look_up(c, tiles[0], tiles[1], t, by_e2))
             first(c, tiles, 2)
             second(c, tiles, 1)
             first(c, tiles, 3)
             second(c, tiles, 2)
             second(c, tiles, 3)
-            before = tiles
-        finish(len(CHUNKS) - 1, join(len(CHUNKS) - 1, before))
+            hid = join(c, tiles)
+        finish(len(CHUNKS) - 1, hid)

@@ -21,8 +21,8 @@ PACK = 4
 K_PASS = P * PACK
 PASSES = K // K_PASS
 LIST_ROWS = 16
-CHUNKS = [256,384,256,128]
-ON_VECTOR = [(0, 3, True), (0, 3, False), (2, 3, True)]
+CHUNKS = [384,256,256,128]
+ON_VECTOR = [(0, 3, True), (0, 3, False)]
 
 
 def tile_picked_yspecmx_bil_p_kernel(
@@ -89,7 +89,8 @@ def tile_picked_yspecmx_bil_p_kernel(
             if o == 0:
                 nc.scalar.copy(out=dst, in_=src)
             else:
-                nc.vector.tensor_copy(out=dst, in_=src)
+                nc.scalar.copy(out=dst[:, :64], in_=src[:, :64])
+                nc.vector.tensor_copy(out=dst[:, 64:], in_=src[:, 64:])
             codes = keep.tile([P, H], U32, name=f"w1_codes{o}", align_bytes=64)
             scales = keep.tile([P, H], U8, name=f"w1_scales{o}", align_bytes=64)
             nc.vector.quantize_mx(out=codes[:].bitcast(FP8X4), scales=scales[:], in_=grouped[:])
@@ -162,7 +163,7 @@ def tile_picked_yspecmx_bil_p_kernel(
             for t, by_e2 in order:
                 if (c, t, by_e2) not in ON_VECTOR:
                     nc.scalar.activation(*look_up(c, z1, y2, t, by_e2), COPY)
-            prod = keep.tile([P, PACK, width], F32, name="prod")
+            prod = ring.tile([P, PACK, width], F32, name="prod")
             return z1, y2, prod, prod
 
         def first(c, tiles, t):
@@ -216,8 +217,6 @@ def tile_picked_yspecmx_bil_p_kernel(
                 if where == c and by_e2:
                     nc.vector.tensor_copy(*look_up(c, tiles[0], tiles[1], t, by_e2))
             first(c, tiles, 0)
-            if hid is not None:
-                finish(c - 1, hid)
             first(c, tiles, 1)
             second(c, tiles, 0)
             for where, t, by_e2 in ON_VECTOR:
@@ -228,5 +227,7 @@ def tile_picked_yspecmx_bil_p_kernel(
             first(c, tiles, 3)
             second(c, tiles, 2)
             second(c, tiles, 3)
+            if hid is not None:
+                finish(c - 1, hid)
             hid = join(c, tiles)
         finish(len(CHUNKS) - 1, hid)

from contextlib import ExitStack

import concourse.mybir as mybir

K, T, S, N, H, U = 1024, 2048, 512, 128, 512, 1024
FLOPS = 2 * K * H * S + 2 * H * N * U

F32 = mybir.dt.float32
BF16 = mybir.dt.bfloat16
I32 = mybir.dt.int32
U32 = mybir.dt.uint32
U16 = mybir.dt.uint16
U8 = mybir.dt.uint8
FP8X4 = mybir.dt.float8_e4m3fn_x4
MULT = mybir.AluOpType.mult
ADD = mybir.AluOpType.add
COPY = mybir.ActivationFunctionType.Copy

P = 128
PACK = 4
K_PASS = P * PACK
PASSES = K // K_PASS
LIST_ROWS = 16
CHUNKS = [384,256,256,128]
ON_VECTOR = [(0, 3, True), (0, 3, False)]


def tile_picked_yspecmx_bil_p_kernel(
    tc, x_words, x_scales, w1, nl, unit, w2, offs, e1, e2, out
):
    nc = tc.nc
    with ExitStack() as ctx:
        keep = ctx.enter_context(tc.tile_pool(name="keep", bufs=1))
        ring = ctx.enter_context(tc.tile_pool(name="ring", bufs=4))
        psum = ctx.enter_context(tc.psum_pool(name="psum", bufs=1))
        psum_out = ctx.enter_context(tc.psum_pool(name="psum_out", bufs=4))

        offs_sb = keep.tile([P, S // LIST_ROWS], U16, name="offs_sb")
        e1_sb = keep.tile([P, U // LIST_ROWS], U16, name="e1_sb")
        e2_sb = keep.tile([P, U // LIST_ROWS], U16, name="e2_sb")

        scale_table = keep.tile([P, T], U8, name="scale_table", align_bytes=64)
        nc.vector.memset(scale_table[:].bitcast(I32), 0)

        w1_raw = []
        for o in range(PASSES):
            raw = keep.tile([P, PACK, H], F32, name=f"w1_raw{o}")
            nc.sync.dma_start(
                out=raw[:], in_=w1[o * K_PASS : (o + 1) * K_PASS, :].rearrange("(p j) c -> p j c", j=PACK)
            )
            w1_raw.append(raw)
            if o == 0:
                nc.sync.dma_start(offs_sb[:], offs)
                for q in range(4):
                    nc.sync.dma_start(
                        out=scale_table[32 * q : 32 * q + 4 * PASSES, :].bitcast(I32),
                        in_=x_scales[:, 4 * q : 4 * q + 4, :].bitcast(I32),
                    )
        word_table = []
        for o in range(PASSES):
            table = keep.tile([P, T], I32, name=f"word_table{o}", align_bytes=64)
            nc.sync.dma_start(out=table[:], in_=x_words[o].rearrange("p n t -> p (n t)").bitcast(I32))
            word_table.append(table)
        nc.sync.dma_start(e2_sb[:], e2)
        nc.sync.dma_start(e1_sb[:], e1)
        unit_sb = keep.tile([P, PACK], F32, name="unit_sb")
        nc.sync.dma_start(out=unit_sb[:], in_=unit.rearrange("(p t) o -> p (t o)", t=PACK))
        w2_raw = keep.tile([P, PACK, N], F32, name="w2_raw")
        nc.sync.dma_start(out=w2_raw[:], in_=w2.rearrange("(p j) n -> p j n", j=PACK))
        starts = [sum(CHUNKS[:c]) for c in range(len(CHUNKS))]
        nl_rows = nl.rearrange("(p t) r -> p t r", t=PACK)
        nl_sb = []
        for c, width in enumerate(CHUNKS):
            if c == 0:
                planes = [keep.tile([P, width], F32, name=f"nl0_{t}", tag=f"nl0_{t}") for t in range(PACK)]
                for t in range(PACK):
                    nc.sync.dma_start(out=planes[t][:], in_=nl_rows[:, t, :width])
                nl_sb.append([plane[:] for plane in planes])
            else:
                share = keep.tile([P, PACK, width], F32, name=f"nl{c}")
                nc.sync.dma_start(out=share[:], in_=nl_rows[:, :, starts[c] : starts[c] + width])
                nl_sb.append([share[:, t, :] for t in range(PACK)])

        w1_codes, w1_scales = [], []
        for o in range(PASSES):
            grouped = keep.tile([P, PACK * H], BF16, name=f"w1_grouped{o}", align_bytes=64)
            dst = grouped[:].rearrange("p (t m j) -> p m t j", t=PACK, j=PACK)
            src = w1_raw[o][:].rearrange("p j (m t) -> p m t j", t=PACK)
            if o == 0:
                nc.scalar.copy(out=dst, in_=src)
            else:
                nc.scalar.copy(out=dst[:, :64], in_=src[:, :64])
                nc.vector.tensor_copy(out=dst[:, 64:], in_=src[:, 64:])
            codes = keep.tile([P, H], U32, name=f"w1_codes{o}", align_bytes=64)
            scales = keep.tile([P, H], U8, name=f"w1_scales{o}", align_bytes=64)
            nc.vector.quantize_mx(out=codes[:].bitcast(FP8X4), scales=scales[:], in_=grouped[:])
            w1_codes.append(codes)
            w1_scales.append(scales)

        x_scale = keep.tile([P, S], U8, name="x_scale", align_bytes=64)
        nc.vector.tensor_copy(x_scale[:], scale_table[:].indirect(offs_sb[:]))

        banks = [psum.tile([P, S], F32, name=f"y_bank{t}") for t in range(PACK)]
        half = S // 2
        picked = {}
        for o in range(PASSES):
            for h in range(2):
                picked[o, h] = keep.tile([P, half], U32, name=f"x_codes{o}_{h}", align_bytes=64)
                nc.vector.tensor_copy(
                    picked[o, h][:],
                    word_table[o][:].bitcast(U32).indirect(offs_sb[:, h * half // LIST_ROWS : (h + 1) * half // LIST_ROWS]),
                )
        steps = [(0, h, t) for h in range(2) for t in range(PACK)]
        steps += [(1, h, t) for t0 in (0, 2) for h in range(2) for t in (t0, t0 + 1)]
        for o, h, t in steps:
            nc.tensor.matmul_mx(
                out=banks[t][:, h * half : (h + 1) * half],
                lhsT=w1_codes[o][:, t * P : (t + 1) * P].bitcast(FP8X4),
                lhsT_scale=w1_scales[o][:, t * P : (t + 1) * P],
                rhs=picked[o, h][:].bitcast(FP8X4),
                rhs_scale=x_scale[4 * o : P, h * half : (h + 1) * half],
                start=(o == 0 and h == 0),
                stop=(o == PASSES - 1 and h == 1),
            )

        w2_grouped = keep.tile([P, PACK * N], BF16, name="w2_grouped", align_bytes=64)
        nc.scalar.copy(
            out=w2_grouped[:].rearrange("p (c i j) -> p c j i", i=4, j=PACK),
            in_=w2_raw[:].rearrange("p j (c i) -> p c j i", i=4),
        )
        w2_codes = keep.tile([P, N], U32, name="w2_codes", align_bytes=64)
        w2_scales = keep.tile([P, N], U8, name="w2_scales", align_bytes=64)

        y = [keep.tile([P, S], F32, name=f"y{t}") for t in range(PACK)]
        z = [keep.tile([P, S], F32, name=f"z{t}") for t in range(PACK)]
        nc.scalar.copy(out=y[0][:, :S], in_=banks[0][:])
        for t in range(PACK):
            if t + 1 < PACK:
                nc.vector.tensor_copy(out=y[t + 1][:, :S], in_=banks[t + 1][:])
            nc.gpsimd.tensor_scalar(z[t][:, :S], y[t][:, :S], unit_sb[:, t : t + 1], 0.0, MULT, ADD)
        nc.vector.quantize_mx(out=w2_codes[:].bitcast(FP8X4), scales=w2_scales[:], in_=w2_grouped[:])

        later = keep.tile([P, 2 * PACK * (U - CHUNKS[0])], F32, name="later", tag="nl0_1")

        def look_up(c, z1, y2, t, by_e2):
            cols = slice(starts[c] // LIST_ROWS, (starts[c] + CHUNKS[c]) // LIST_ROWS)
            if by_e2:
                return y2[:, t, :], y[t][:].indirect(e2_sb[:, cols])
            return z1[:, t, :], z[t][:].indirect(e1_sb[:, cols])

        def fetch(c):
            width = CHUNKS[c]
            if c == 0:
                z1 = keep.tile([P, PACK, width], F32, name="z1_first")[:]
                y2 = keep.tile([P, PACK, width], F32, name="y2_first")[:]
            else:
                at = 2 * PACK * (starts[c] - CHUNKS[0])
                z1 = later[:, at : at + PACK * width].rearrange("p (t r) -> p t r", t=PACK)
                y2 = later[:, at + PACK * width : at + 2 * PACK * width].rearrange("p (t r) -> p t r", t=PACK)
            order = [(0, True), (1, True), (0, False), (1, False), (2, True), (2, False), (3, True), (3, False)]
            if c > 0:
                order = [(t, second) for t in range(PACK) for second in (False, True)]
            for t, by_e2 in order:
                if (c, t, by_e2) not in ON_VECTOR:
                    nc.scalar.activation(*look_up(c, z1, y2, t, by_e2), COPY)
            prod = ring.tile([P, PACK, width], F32, name="prod")
            return z1, y2, prod, prod

        def first(c, tiles, t):
            z1, y2, prod, rest = tiles
            nc.vector.tensor_tensor(prod[:, t, :], z1[:, t, :], nl_sb[c][t], MULT)

        def second(c, tiles, t):
            z1, y2, prod, rest = tiles
            nc.vector.scalar_tensor_tensor(
                rest[:, t, :], prod[:, t, :], unit_sb[:, t : t + 1], y2[:, t, :], ADD, MULT
            )

        def join(c, tiles):
            z1, y2, prod, rest = tiles
            hid = ring.tile([P, PACK * CHUNKS[c]], BF16, name="hid", align_bytes=64)
            nc.vector.tensor_tensor(
                hid[:].rearrange("p (c i t) -> p c t i", i=4, t=PACK),
                z1.rearrange("p t (c i) -> p c t i", i=4),
                rest[:].rearrange("p t (c i) -> p c t i", i=4),
                ADD,
            )
            return hid

        def finish(c, hid):
            width = CHUNKS[c]
            codes = ring.tile([P, width], U32, name="hid_codes", align_bytes=64)
            scales = ring.tile([P, width], U8, name="hid_scales", align_bytes=64)
            nc.vector.quantize_mx(out=codes[:].bitcast(FP8X4), scales=scales[:], in_=hid[:])
            acc = psum_out.tile([P, width], F32, name="acc")
            lo = 0
            for part in (512, 256, 128):
                if width - lo >= part:
                    nc.tensor.matmul_mx(
                        out=acc[:, lo : lo + part],
                        lhsT=w2_codes[:].bitcast(FP8X4),
                        lhsT_scale=w2_scales[:],
                        rhs=codes[:, lo : lo + part].bitcast(FP8X4),
                        rhs_scale=scales[:, lo : lo + part],
                        start=True,
                        stop=True,
                    )
                    lo = lo + part
            result = ring.tile([P, width], F32, name="result")
            nc.scalar.copy(out=result[:], in_=acc[:])
            nc.sync.dma_start(out=out[:, starts[c] : starts[c] + width], in_=result[:])

        hid = None
        for c in range(len(CHUNKS)):
            tiles = fetch(c)
            for where, t, by_e2 in ON_VECTOR:
                if where == c and by_e2:
                    nc.vector.tensor_copy(*look_up(c, tiles[0], tiles[1], t, by_e2))
            first(c, tiles, 0)
            first(c, tiles, 1)
            second(c, tiles, 0)
            for where, t, by_e2 in ON_VECTOR:
                if where == c and not by_e2:
                    nc.vector.tensor_copy(*look_up(c, tiles[0], tiles[1], t, by_e2))
            first(c, tiles, 2)
            second(c, tiles, 1)
            first(c, tiles, 3)
            second(c, tiles, 2)
            second(c, tiles, 3)
            if hid is not None:
                finish(c - 1, hid)
            hid = join(c, tiles)
        finish(len(CHUNKS) - 1, hid)
